import numpy as np
import ml_dtypes


def mxq(x, axis, fmt="e4m3"):
    dtype, down = {"e4m3": (ml_dtypes.float8_e4m3fn, 7), "e5m2": (ml_dtypes.float8_e5m2, 14)}[fmt]
    v = np.moveaxis(np.asarray(x, np.float32).astype(ml_dtypes.bfloat16).astype(np.float64), axis, -1)
    blocks = v.reshape(v.shape[:-1] + (-1, 32))
    amax = np.abs(blocks).max(-1, keepdims=True)
    byte = np.maximum(np.where(amax > 0, np.frexp(amax)[1] - 1 + 127, 0) - down, 1)
    scale = np.exp2(byte - 127.0)
    codes = (blocks / scale).astype(np.float32).astype(dtype).astype(np.float64)
    return np.moveaxis((codes * scale).reshape(v.shape), -1, axis)


WIDE = False


def mx_kscale(k):
    if not WIDE:
        return np.ones(k)
    levels = np.array([10, -10, 5, -5, 0])
    if k % 512:
        return np.exp2(np.random.permutation(np.resize(levels, k // 32))).repeat(32)
    a = np.empty((k // 512, 16))
    for p in range(k // 512):
        a[p, :8] = np.random.permutation(np.resize(levels, 8))
        for g in range(8):
            far = levels[np.abs(levels - a[p, g]) >= 10]
            a[p, g + 8] = far[np.random.randint(len(far))]
    return np.exp2(a.ravel()).repeat(32)


def f64(x):
    return np.asarray(x).astype(np.float64)


def striped(idx):
    return np.tile(np.asarray(idx).reshape(-1, 16).T, (8, 1)).astype(np.uint16)


def unstriped(offs):
    return offs[:16].T.reshape(-1).astype(np.int64)


E2M1 = np.array([0.0, 0.5, 1.0, 1.5, 2.0, 3.0, 4.0, 6.0, -0.0, -0.5, -1.0, -1.5, -2.0, -3.0, -4.0, -6.0])


def pack_weight(w, fmt):
    k, n = w.shape
    w = f64(np.asarray(w, np.float32).astype(ml_dtypes.bfloat16)).reshape(k // 32, 32, n)
    amax = np.abs(w).max(1)
    if fmt == "e4m3":
        byte = np.frexp(amax)[1] - 1 + 127 - 7
    else:
        mant, ex = np.frexp(amax / 6.0)
        byte = np.where(mant > 0.5, ex, ex - 1) + 127
    byte = np.clip(np.where(amax > 0, byte, 1), 1, 254)
    scaled = (w * np.exp2(127.0 - byte)[:, None, :]).reshape(k, n).astype(np.float32)
    by_word = np.ascontiguousarray(scaled.reshape(k // 512, 128, 4, n).transpose(0, 1, 3, 2))
    if fmt == "e4m3":
        words = by_word.astype(ml_dtypes.float8_e4m3fn).view(np.uint8)
    else:
        c = by_word.astype(ml_dtypes.float4_e2m1fn).view(np.uint8) & 0xF
        words = (c[..., 0::2] | (c[..., 1::2] << 4)).reshape(k // 512, 128, 2 * n)
    return np.ascontiguousarray(words), np.ascontiguousarray(byte.astype(np.uint8).reshape(k // 512, 16, n))


def unpack_weight(words, scales, fmt):
    g, _, n = scales.shape
    words = np.ascontiguousarray(words).reshape(g, 128, n, -1)
    if fmt == "e4m3":
        vals = words.view(ml_dtypes.float8_e4m3fn).astype(np.float64)
    else:
        nib = np.empty((g, 128, n, 4), np.uint8)
        nib[..., 0::2] = words & 0xF
        nib[..., 1::2] = words >> 4
        vals = E2M1[nib]
    vals = vals * np.repeat(np.exp2(scales.astype(np.float64) - 127.0), 8, axis=1)[..., None]
    return vals.transpose(0, 1, 3, 2).reshape(g * 512, n)


K, R, F, T, J, G = 512, 128, 512, 2048, 512, 32


def setup_inputs():
    n = np.random.standard_normal
    idx = np.random.permutation(T)[:J]
    fk = mx_kscale(K)
    dtabp = pack_weight(n((K, T)) / fk[:, None], "e2m1")
    tabp = pack_weight(n((K, T)) / fk[:, None], "e2m1")
    return {
        "dtab_words": dtabp[0],
        "dtab_scales": dtabp[1],
        "tab_words": tabp[0],
        "tab_scales": tabp[1],
        "w1": (n((K, R)) * 1 / np.sqrt(K) * fk[:, None]).astype(np.float32),
        "sharp": (np.random.uniform(0.3, 1.5, (R, 1))).astype(np.float32),
        "og": (np.random.uniform(0.5, 2.0, (R, 1))).astype(np.float32),
        "base": (0.3 * n((R, J))).astype(np.float32),
        "offs": striped(idx),
    }


def reference(dtab_words, dtab_scales, tab_words, tab_scales, w1, sharp, og, base, offs):
    idx = unstriped(offs)
    dtabu = unpack_weight(dtab_words, dtab_scales, "e2m1")
    tabu = unpack_weight(tab_words, tab_scales, "e2m1")
    w1q = mxq(f64(w1), 0, "e4m3")
    tabidxg = tabu[:, idx]
    a = w1q.T @ tabidxg
    dtabidxg = dtabu[:, idx]
    ta = w1q.T @ dtabidxg
    m1 = a.reshape(R, G, J // G).mean(axis=2)
    mr = np.repeat(m1, J // G, axis=1)
    ce = a - mr
    tm1 = ta.reshape(R, G, J // G).mean(axis=2)
    tmr = np.repeat(tm1, J // G, axis=1)
    tce = ta - tmr
    tu1 = (ta - tce * ce * 2.0 * f64(sharp) * a / (np.square(ce) * f64(sharp) + 1.0)) / (np.square(ce) * f64(sharp) + 1.0)
    y = tu1 * f64(og) + f64(base)
    return y

@@ -1,0 +1,159 @@
+from contextlib import ExitStack
+
+import concourse.mybir as mybir
+
+K, R, T, J, G = 512, 128, 2048, 512, 32
+P = 128
+PACK = 4
+GROUP = J // G
+HALVES = 2
+HJ = J // HALVES
+HG = G // HALVES
+FLOPS = 2 * 2 * K * R * J
+
+F32 = mybir.dt.float32
+BF16 = mybir.dt.bfloat16
+I32 = mybir.dt.int32
+U32 = mybir.dt.uint32
+U16 = mybir.dt.uint16
+U8 = mybir.dt.uint8
+FP8X4 = mybir.dt.float8_e4m3fn_x4
+FP4X4 = mybir.dt.float4_e2m1fn_x4
+ALU = mybir.AluOpType
+ACT = mybir.ActivationFunctionType
+AX = mybir.AxisListType
+
+
+def tile_attend_tcontrastpool_kernel(tc, dtab_words, dtab_scales, tab_words, tab_scales, w1, sharp, og, base, offs, out):
+    nc = tc.nc
+    with ExitStack() as ctx:
+        sb = ctx.enter_context(tc.tile_pool(name="sb", bufs=1))
+        ps = ctx.enter_context(tc.psum_pool(name="ps", bufs=1))
+
+        def halves(name):
+            return [sb.tile([P, HJ], F32, name="%s%d" % (name, h)) for h in range(HALVES)]
+
+        def grouped(ap):
+            return ap.rearrange("p (g i) -> p g i", i=GROUP)
+
+        def spread(ap):
+            return ap.unsqueeze(2).to_broadcast([P, HG, GROUP])
+
+        offsets = sb.tile([P, J // 16], U16, name="offsets")
+        nc.sync.dma_start(offsets[:], offs)
+
+        tw = sb.tile([P, T], U16, name="tw")
+        dw = sb.tile([P, T], U16, name="dw")
+        ts = sb.tile([P, T], U8, name="ts")
+        ds = sb.tile([P, T], U8, name="ds", tag="late")
+        w_raw = sb.tile([P, PACK * R], F32, name="w_raw", tag="stage")
+        s_col = sb.tile([P, 1], F32, name="s_col")
+        og_col = sb.tile([P, 1], F32, name="og_col")
+
+        nc.vector.memset(ts[:].bitcast(I32), 0)
+        nc.vector.memset(ds[:].bitcast(I32), 0)
+        warm_in = sb.tile([P, 1], F32, name="warm_in")
+        warm_out = sb.tile([P, 1], F32, name="warm_out")
+        nc.vector.memset(warm_in[:], 1.0)
+
+        nc.sync.dma_start(w_raw[:], w1.rearrange("(p j) r -> p (j r)", j=PACK))
+        nc.sync.dma_start(tw[:].bitcast(I32), tab_words[0].bitcast(I32))
+        nc.sync.dma_start(dw[:].bitcast(I32), dtab_words[0].bitcast(I32))
+        for q in (0, 2, 1, 3):
+            nc.scalar.dma_start(ts[32 * q:32 * q + 4, :].bitcast(I32), tab_scales[0, 4 * q:4 * q + 4, :].bitcast(I32))
+        for q in (0, 2, 1, 3):
+            nc.sync.dma_start(ds[32 * q:32 * q + 4, :].bitcast(I32), dtab_scales[0, 4 * q:4 * q + 4, :].bitcast(I32))
+        nc.gpsimd.dma_start(s_col[:], sharp)
+        nc.gpsimd.dma_start(og_col[:], og)
+
+        nc.scalar.activation(warm_out[:], warm_in[:], ACT.Abs_reciprocal_sqrt)
+
+        w_bf = sb.tile([P, R, PACK], BF16, name="w_bf", align_bytes=64)
+        nc.scalar.copy(w_bf[:], w_raw[:].rearrange("p (j r) -> p r j", j=PACK))
+        base_sb = sb.tile([P, J], F32, name="base_sb", tag="stage")
+        nc.sync.dma_start(base_sb[:], base)
+
+        neg_s = sb.tile([P, 1], F32, name="neg_s")
+        s_mean = sb.tile([P, 1], F32, name="s_mean")
+        nc.gpsimd.tensor_scalar(neg_s[:], s_col[:], -1.0, 0.0, ALU.mult, ALU.add)
+        nc.gpsimd.tensor_scalar(s_mean[:], s_col[:], 1.0 / (GROUP * GROUP), 0.0, ALU.mult, ALU.add)
+
+        gtw = sb.tile([P, J], U16, name="gtw", align_bytes=64)
+        gts = sb.tile([P, J], U8, name="gts", align_bytes=64)
+        gdw = sb.tile([P, J], U16, name="gdw", align_bytes=64)
+        gds = sb.tile([P, J], U8, name="gds", align_bytes=64)
+        w_codes = sb.tile([P, R], U32, name="w_codes", align_bytes=64)
+        w_scales = sb.tile([P, R], U8, name="w_scales", align_bytes=64)
+
+        nc.vector.tensor_copy(gts[:], ts[:].indirect(offsets[:]))
+        nc.vector.quantize_mx(out=w_codes[:].bitcast(FP8X4), scales=w_scales[:],
+                              in_=w_bf[:].rearrange("p r j -> p (r j)"))
+        nc.vector.tensor_copy(gtw[:], tw[:].indirect(offsets[:]))
+        nc.vector.tensor_copy(gdw[:], dw[:].indirect(offsets[:]))
+        nc.vector.tensor_copy(gds[:], ds[:].indirect(offsets[:]))
+
+        def product(name, words, scales):
+            banks = []
+            for h in range(HALVES):
+                cols = slice(h * HJ, (h + 1) * HJ)
+                bank = ps.tile([P, HJ], F32, name="%s%d" % (name, h))
+                nc.tensor.matmul_mx(out=bank[:], lhsT=w_codes[:].bitcast(FP8X4), lhsT_scale=w_scales[:],
+                                    rhs=words[:, cols].bitcast(FP4X4), rhs_scale=scales[:, cols],
+                                    start=True, stop=True)
+                banks.append(bank)
+            return banks
+
+        a = product("a", gtw, gts)
+        ta = product("ta", gdw, gds)
+        hs = range(HALVES)
+
+        a_sq, x, e0 = halves("a_sq"), halves("x"), halves("e0")
+        ce, sq, den = halves("ce"), halves("sq"), halves("den")
+        q1, q2, q4 = halves("q1"), halves("q2"), halves("q4")
+        tce, u, v, n, y1, y = halves("tce"), halves("u"), halves("v"), halves("n"), halves("y1"), halves("y")
+        a_sums = sb.tile([P, G], F32, name="a_sums", tag="late")
+        a_sum = [a_sums[:, h * HG:(h + 1) * HG] for h in hs]
+        t_sum = [sb.tile([P, HG], F32, name="t_sum%d" % h) for h in hs]
+        sm2 = [sb.tile([P, HG], F32, name="sm2_%d" % h) for h in hs]
+
+        for h in hs:
+            nc.scalar.activation(a_sq[h][:], a[h][:], ACT.Square)
+        for h in hs:
+            nc.scalar.activation(x[h][:], a_sq[h][:], ACT.Identity, bias=1.0, scale=neg_s[:])
+        for h in hs:
+            nc.vector.tensor_reduce(a_sum[h], grouped(a[h][:]), AX.X, ALU.add)
+        for h in hs:
+            nc.vector.scalar_tensor_tensor(sm2[h][:], a_sum[h], s_mean[:], a_sum[h], ALU.mult, ALU.mult)
+        for h in hs:
+            nc.vector.scalar_tensor_tensor(grouped(ce[h][:]), spread(a_sum[h]), -1.0 / GROUP, grouped(a[h][:]),
+                                           ALU.mult, ALU.add)
+        for h in hs:
+            nc.gpsimd.tensor_tensor(grouped(e0[h][:]), grouped(x[h][:]), spread(sm2[h][:]), ALU.add)
+        for h in hs:
+            nc.scalar.activation(sq[h][:], ce[h][:], ACT.Square)
+        for h in hs:
+            nc.scalar.activation(den[h][:], sq[h][:], ACT.Identity, bias=1.0, scale=s_col[:])
+        for h in hs:
+            nc.scalar.activation(q1[h][:], den[h][:], ACT.Abs_reciprocal_sqrt)
+        for h in hs:
+            nc.scalar.activation(q2[h][:], q1[h][:], ACT.Square)
+        for h in hs:
+            nc.scalar.activation(q4[h][:], q2[h][:], ACT.Square)
+        for h in hs:
+            nc.vector.tensor_reduce(t_sum[h][:], grouped(ta[h][:]), AX.X, ALU.add)
+        for h in hs:
+            nc.vector.scalar_tensor_tensor(grouped(tce[h][:]), spread(t_sum[h][:]), -1.0 / GROUP, grouped(ta[h][:]),
+                                           ALU.mult, ALU.add)
+        for h in hs:
+            nc.vector.tensor_tensor(u[h][:], tce[h][:], e0[h][:], ALU.mult)
+        for h in hs:
+            nc.vector.scalar_tensor_tensor(grouped(v[h][:]), spread(t_sum[h][:]), 1.0 / GROUP, grouped(den[h][:]),
+                                           ALU.mult, ALU.mult)
+        for h in hs:
+            nc.vector.tensor_tensor(n[h][:], u[h][:], v[h][:], ALU.add)
+        for h in hs:
+            nc.vector.scalar_tensor_tensor(y1[h][:], n[h][:], og_col[:], q4[h][:], ALU.mult, ALU.mult)
+        for h in hs:
+            cols = slice(h * HJ, (h + 1) * HJ)
+            nc.vector.tensor_tensor(y[h][:], y1[h][:], base_sb[:, cols], ALU.add)
+            nc.sync.dma_start(out[:, cols], y[h][:])

@@ -42,93 +42,89 @@ def tile_attend_tcontrastpool_kernel(tc, dtab_words, dtab_scales, tab_words, tab
         offsets = sb.tile([P, J // 16], U16, name="offsets")
         nc.sync.dma_start(offsets[:], offs)
 
-        tw = sb.tile([P, T], U16, name="tw")
-        dw = sb.tile([P, T], U16, name="dw")
+        tw = sb.tile([P, T], U16, name="tw", tag="after_words")
         ts = sb.tile([P, T], U8, name="ts")
-        ds = sb.tile([P, T], U8, name="ds", tag="late")
-        w_raw = sb.tile([P, PACK * R], F32, name="w_raw", tag="stage")
+        ds = sb.tile([P, T], U8, name="ds")
         s_col = sb.tile([P, 1], F32, name="s_col")
         og_col = sb.tile([P, 1], F32, name="og_col")
 
         nc.vector.memset(ts[:].bitcast(I32), 0)
         nc.vector.memset(ds[:].bitcast(I32), 0)
-        warm_in = sb.tile([P, 1], F32, name="warm_in")
-        warm_out = sb.tile([P, 1], F32, name="warm_out")
+        warm_in = sb.tile([P, 1], F32, name="warm_in", tag="after_warm_in")
+        warm_out = sb.tile([P, 1], F32, name="warm_out", tag="after_warm_out")
         nc.vector.memset(warm_in[:], 1.0)
 
-        nc.sync.dma_start(w_raw[:], w1.rearrange("(p j) r -> p (j r)", j=PACK))
         nc.sync.dma_start(tw[:].bitcast(I32), tab_words[0].bitcast(I32))
-        nc.sync.dma_start(dw[:].bitcast(I32), dtab_words[0].bitcast(I32))
         for q in (0, 2, 1, 3):
-            nc.scalar.dma_start(ts[32 * q:32 * q + 4, :].bitcast(I32), tab_scales[0, 4 * q:4 * q + 4, :].bitcast(I32))
+            nc.sync.dma_start(ts[32 * q:32 * q + 4, :].bitcast(I32), tab_scales[0, 4 * q:4 * q + 4, :].bitcast(I32))
         for q in (0, 2, 1, 3):
             nc.sync.dma_start(ds[32 * q:32 * q + 4, :].bitcast(I32), dtab_scales[0, 4 * q:4 * q + 4, :].bitcast(I32))
         nc.gpsimd.dma_start(s_col[:], sharp)
         nc.gpsimd.dma_start(og_col[:], og)
 
         nc.scalar.activation(warm_out[:], warm_in[:], ACT.Abs_reciprocal_sqrt)
+        w_raw = sb.tile([P, PACK * R], F32, name="w_raw", tag="after_warm_in")
+        dw = sb.tile([P, T], U16, name="dw", tag="after_warm_out")
+        nc.scalar.dma_start(w_raw[:], w1.rearrange("(p j) r -> p (j r)", j=PACK))
+        nc.sync.dma_start(dw[:].bitcast(I32), dtab_words[0].bitcast(I32))
 
-        w_bf = sb.tile([P, R, PACK], BF16, name="w_bf", align_bytes=64)
+        w_bf = sb.tile([P, R, PACK], BF16, name="w_bf", tag="after_quant", align_bytes=64)
         nc.scalar.copy(w_bf[:], w_raw[:].rearrange("p (j r) -> p r j", j=PACK))
-        base_sb = sb.tile([P, J], F32, name="base_sb", tag="stage")
-        nc.sync.dma_start(base_sb[:], base)
-
-        neg_s = sb.tile([P, 1], F32, name="neg_s")
-        s_mean = sb.tile([P, 1], F32, name="s_mean")
-        nc.gpsimd.tensor_scalar(neg_s[:], s_col[:], -1.0, 0.0, ALU.mult, ALU.add)
-        nc.gpsimd.tensor_scalar(s_mean[:], s_col[:], 1.0 / (GROUP * GROUP), 0.0, ALU.mult, ALU.add)
 
         gtw = sb.tile([P, J], U16, name="gtw", align_bytes=64)
         gts = sb.tile([P, J], U8, name="gts", align_bytes=64)
-        gdw = sb.tile([P, J], U16, name="gdw", align_bytes=64)
-        gds = sb.tile([P, J], U8, name="gds", align_bytes=64)
         w_codes = sb.tile([P, R], U32, name="w_codes", align_bytes=64)
         w_scales = sb.tile([P, R], U8, name="w_scales", align_bytes=64)
 
+        nc.vector.tensor_copy(gtw[:], tw[:].indirect(offsets[:]))
         nc.vector.tensor_copy(gts[:], ts[:].indirect(offsets[:]))
         nc.vector.quantize_mx(out=w_codes[:].bitcast(FP8X4), scales=w_scales[:],
                               in_=w_bf[:].rearrange("p r j -> p (r j)"))
-        nc.vector.tensor_copy(gtw[:], tw[:].indirect(offsets[:]))
-        nc.vector.tensor_copy(gdw[:], dw[:].indirect(offsets[:]))
+        gds = sb.tile([P, J], U8, name="gds", tag="after_quant", align_bytes=64)
         nc.vector.tensor_copy(gds[:], ds[:].indirect(offsets[:]))
+        base_sb = sb.tile([P, J], F32, name="base_sb", tag="after_words")
+        nc.sync.dma_start(base_sb[:], base)
 
         def product(name, words, scales):
-            banks = []
-            for h in range(HALVES):
-                cols = slice(h * HJ, (h + 1) * HJ)
-                bank = ps.tile([P, HJ], F32, name="%s%d" % (name, h))
-                nc.tensor.matmul_mx(out=bank[:], lhsT=w_codes[:].bitcast(FP8X4), lhsT_scale=w_scales[:],
-                                    rhs=words[:, cols].bitcast(FP4X4), rhs_scale=scales[:, cols],
-                                    start=True, stop=True)
-                banks.append(bank)
-            return banks
+            bank = ps.tile([P, HJ], F32, name=name)
+            nc.tensor.matmul_mx(out=bank[:], lhsT=w_codes[:].bitcast(FP8X4), lhsT_scale=w_scales[:],
+                                rhs=words.bitcast(FP4X4), rhs_scale=scales, start=True, stop=True)
+            return bank
 
-        a = product("a", gtw, gts)
-        ta = product("ta", gdw, gds)
+        def cols(h):
+            return slice(h * HJ, (h + 1) * HJ)
+
+        a = [product("a%d" % h, gtw[:, cols(h)], gts[:, cols(h)]) for h in range(HALVES)]
         hs = range(HALVES)
 
         a_sq, x, e0 = halves("a_sq"), halves("x"), halves("e0")
         ce, sq, den = halves("ce"), halves("sq"), halves("den")
         q1, q2, q4 = halves("q1"), halves("q2"), halves("q4")
         tce, u, v, n, y1, y = halves("tce"), halves("u"), halves("v"), halves("n"), halves("y1"), halves("y")
-        a_sums = sb.tile([P, G], F32, name="a_sums", tag="late")
-        a_sum = [a_sums[:, h * HG:(h + 1) * HG] for h in hs]
+        a_sum = [sb.tile([P, HG], F32, name="a_sum%d" % h, tag="after_mean%d" % h, align_bytes=64) for h in hs]
         t_sum = [sb.tile([P, HG], F32, name="t_sum%d" % h) for h in hs]
+        m2 = [sb.tile([P, HG], F32, name="m2_%d" % h) for h in hs]
         sm2 = [sb.tile([P, HG], F32, name="sm2_%d" % h) for h in hs]
 
         for h in hs:
             nc.scalar.activation(a_sq[h][:], a[h][:], ACT.Square)
         for h in hs:
-            nc.scalar.activation(x[h][:], a_sq[h][:], ACT.Identity, bias=1.0, scale=neg_s[:])
+            nc.scalar.activation(x[h][:], a_sq[h][:], ACT.Copy, scale=s_col[:])
         for h in hs:
-            nc.vector.tensor_reduce(a_sum[h], grouped(a[h][:]), AX.X, ALU.add)
+            nc.vector.tensor_reduce(a_sum[h][:], grouped(a[h][:]), AX.X, ALU.add)
         for h in hs:
-            nc.vector.scalar_tensor_tensor(sm2[h][:], a_sum[h], s_mean[:], a_sum[h], ALU.mult, ALU.mult)
+            nc.scalar.activation(m2[h][:], a_sum[h][:], ACT.Square, scale=1.0 / GROUP)
+            nc.scalar.activation(sm2[h][:], m2[h][:], ACT.Identity, bias=1.0, scale=s_col[:])
         for h in hs:
-            nc.vector.scalar_tensor_tensor(grouped(ce[h][:]), spread(a_sum[h]), -1.0 / GROUP, grouped(a[h][:]),
+            nc.vector.scalar_tensor_tensor(grouped(ce[h][:]), spread(a_sum[h][:]), -1.0 / GROUP, grouped(a[h][:]),
                                            ALU.mult, ALU.add)
+        ta = []
         for h in hs:
-            nc.gpsimd.tensor_tensor(grouped(e0[h][:]), grouped(x[h][:]), spread(sm2[h][:]), ALU.add)
+            gdw = sb.tile([P, HJ], U16, name="gdw%d" % h, tag="after_mean%d" % h, align_bytes=64)
+            nc.vector.tensor_copy(gdw[:], dw[:].indirect(offsets[:, h * HG:(h + 1) * HG]))
+            ta.append(product("ta%d" % h, gdw[:], gds[:, cols(h)]))
+        for h in hs:
+            nc.gpsimd.tensor_tensor(grouped(e0[h][:]), spread(sm2[h][:]), grouped(x[h][:]), ALU.subtract)
         for h in hs:
             nc.scalar.activation(sq[h][:], ce[h][:], ACT.Square)
         for h in hs:
@@ -154,6 +150,5 @@ def tile_attend_tcontrastpool_kernel(tc, dtab_words, dtab_scales, tab_words, tab
         for h in hs:
             nc.vector.scalar_tensor_tensor(y1[h][:], n[h][:], og_col[:], q4[h][:], ALU.mult, ALU.mult)
         for h in hs:
-            cols = slice(h * HJ, (h + 1) * HJ)
-            nc.vector.tensor_tensor(y[h][:], y1[h][:], base_sb[:, cols], ALU.add)
-            nc.sync.dma_start(out[:, cols], y[h][:])
+            nc.vector.tensor_tensor(y[h][:], y1[h][:], base_sb[:, cols(h)], ALU.add)
+            nc.sync.dma_start(out[:, cols(h)], y[h][:])

@@ -39,51 +39,54 @@ def tile_attend_tcontrastpool_kernel(tc, dtab_words, dtab_scales, tab_words, tab
         def spread(ap):
             return ap.unsqueeze(2).to_broadcast([P, HG, GROUP])
 
+        def cols(h):
+            return slice(h * HJ, (h + 1) * HJ)
+
+        def load_scales(queue, tile, scales):
+            for q in (0, 2, 1, 3):
+                queue.dma_start(tile[32 * q:32 * q + 4, :].bitcast(I32), scales[0, 4 * q:4 * q + 4, :].bitcast(I32))
+
+        hs = range(HALVES)
         offsets = sb.tile([P, J // 16], U16, name="offsets")
         nc.sync.dma_start(offsets[:], offs)
 
-        tw = sb.tile([P, T], U16, name="tw", tag="after_words")
+        tw = sb.tile([P, T], U16, name="tw", tag="words")
         ts = sb.tile([P, T], U8, name="ts")
-        ds = sb.tile([P, T], U8, name="ds")
         s_col = sb.tile([P, 1], F32, name="s_col")
         og_col = sb.tile([P, 1], F32, name="og_col")
+        warm_in = sb.tile([P, 1], F32, name="warm_in", tag="after_warm_in")
+        warm_out = sb.tile([P, 1], F32, name="warm_out", tag="after_warm_out", align_bytes=64)
 
         nc.vector.memset(ts[:].bitcast(I32), 0)
-        nc.vector.memset(ds[:].bitcast(I32), 0)
-        warm_in = sb.tile([P, 1], F32, name="warm_in", tag="after_warm_in")
-        warm_out = sb.tile([P, 1], F32, name="warm_out", tag="after_warm_out")
         nc.vector.memset(warm_in[:], 1.0)
-
         nc.sync.dma_start(tw[:].bitcast(I32), tab_words[0].bitcast(I32))
-        for q in (0, 2, 1, 3):
-            nc.sync.dma_start(ts[32 * q:32 * q + 4, :].bitcast(I32), tab_scales[0, 4 * q:4 * q + 4, :].bitcast(I32))
-        for q in (0, 2, 1, 3):
-            nc.sync.dma_start(ds[32 * q:32 * q + 4, :].bitcast(I32), dtab_scales[0, 4 * q:4 * q + 4, :].bitcast(I32))
+        load_scales(nc.sync, ts, tab_scales)
         nc.gpsimd.dma_start(s_col[:], sharp)
         nc.gpsimd.dma_start(og_col[:], og)
 
         nc.scalar.activation(warm_out[:], warm_in[:], ACT.Abs_reciprocal_sqrt)
         w_raw = sb.tile([P, PACK * R], F32, name="w_raw", tag="after_warm_in")
-        dw = sb.tile([P, T], U16, name="dw", tag="after_warm_out")
-        nc.scalar.dma_start(w_raw[:], w1.rearrange("(p j) r -> p (j r)", j=PACK))
-        nc.sync.dma_start(dw[:].bitcast(I32), dtab_words[0].bitcast(I32))
+        nc.sync.dma_start(w_raw[:], w1.rearrange("(p j) r -> p (j r)", j=PACK))
+        ds = sb.tile([P, T], U8, name="ds", tag="after_warm_out", align_bytes=64)
+        nc.vector.memset(ds[:].bitcast(I32), 0)
+        load_scales(nc.scalar, ds, dtab_scales)
 
-        w_bf = sb.tile([P, R, PACK], BF16, name="w_bf", tag="after_quant", align_bytes=64)
+        w_bf = sb.tile([P, R, PACK], BF16, name="w_bf", align_bytes=64)
         nc.scalar.copy(w_bf[:], w_raw[:].rearrange("p (j r) -> p r j", j=PACK))
 
-        gtw = sb.tile([P, J], U16, name="gtw", align_bytes=64)
+        gtw = sb.tile([P, J], U16, name="gtw", tag="after_a", align_bytes=64)
         gts = sb.tile([P, J], U8, name="gts", align_bytes=64)
         w_codes = sb.tile([P, R], U32, name="w_codes", align_bytes=64)
         w_scales = sb.tile([P, R], U8, name="w_scales", align_bytes=64)
 
         nc.vector.tensor_copy(gtw[:], tw[:].indirect(offsets[:]))
+        dw = sb.tile([P, T], U16, name="dw", tag="words")
+        nc.sync.dma_start(dw[:].bitcast(I32), dtab_words[0].bitcast(I32))
         nc.vector.tensor_copy(gts[:], ts[:].indirect(offsets[:]))
         nc.vector.quantize_mx(out=w_codes[:].bitcast(FP8X4), scales=w_scales[:],
                               in_=w_bf[:].rearrange("p r j -> p (r j)"))
-        gds = sb.tile([P, J], U8, name="gds", tag="after_quant", align_bytes=64)
+        gds = sb.tile([P, J], U8, name="gds", align_bytes=64)
         nc.vector.tensor_copy(gds[:], ds[:].indirect(offsets[:]))
-        base_sb = sb.tile([P, J], F32, name="base_sb", tag="after_words")
-        nc.sync.dma_start(base_sb[:], base)
 
         def product(name, words, scales):
             bank = ps.tile([P, HJ], F32, name=name)
@@ -91,42 +94,34 @@ def tile_attend_tcontrastpool_kernel(tc, dtab_words, dtab_scales, tab_words, tab
                                 rhs=words.bitcast(FP4X4), rhs_scale=scales, start=True, stop=True)
             return bank
 
-        def cols(h):
-            return slice(h * HJ, (h + 1) * HJ)
+        a = [product("a%d" % h, gtw[:, cols(h)], gts[:, cols(h)]) for h in hs]
+        base_sb = sb.tile([P, J], F32, name="base_sb", tag="after_a", align_bytes=64)
+        nc.sync.dma_start(base_sb[:], base)
 
-        a = [product("a%d" % h, gtw[:, cols(h)], gts[:, cols(h)]) for h in range(HALVES)]
-        hs = range(HALVES)
-
-        a_sq, x, e0 = halves("a_sq"), halves("x"), halves("e0")
-        ce, sq, den = halves("ce"), halves("sq"), halves("den")
+        a_sb = sb.tile([P, J], F32, name="a_sb")
+        ce = sb.tile([P, J], F32, name="ce")
+        sq, den = halves("sq"), halves("den")
         q1, q2, q4 = halves("q1"), halves("q2"), halves("q4")
         tce, u, v, n, y1, y = halves("tce"), halves("u"), halves("v"), halves("n"), halves("y1"), halves("y")
-        a_sum = [sb.tile([P, HG], F32, name="a_sum%d" % h, tag="after_mean%d" % h, align_bytes=64) for h in hs]
+        a_sum = [sb.tile([P, HG], F32, name="a_sum%d" % h, tag="after_mean%d" % h, align_bytes=64)[:] for h in hs]
         t_sum = [sb.tile([P, HG], F32, name="t_sum%d" % h) for h in hs]
-        m2 = [sb.tile([P, HG], F32, name="m2_%d" % h) for h in hs]
-        sm2 = [sb.tile([P, HG], F32, name="sm2_%d" % h) for h in hs]
 
         for h in hs:
-            nc.scalar.activation(a_sq[h][:], a[h][:], ACT.Square)
+            nc.scalar.copy(a_sb[:, cols(h)], a[h][:])
         for h in hs:
-            nc.scalar.activation(x[h][:], a_sq[h][:], ACT.Copy, scale=s_col[:])
+            nc.vector.tensor_reduce(a_sum[h], grouped(a[h][:]), AX.X, ALU.add)
         for h in hs:
-            nc.vector.tensor_reduce(a_sum[h][:], grouped(a[h][:]), AX.X, ALU.add)
-        for h in hs:
-            nc.scalar.activation(m2[h][:], a_sum[h][:], ACT.Square, scale=1.0 / GROUP)
-            nc.scalar.activation(sm2[h][:], m2[h][:], ACT.Identity, bias=1.0, scale=s_col[:])
-        for h in hs:
-            nc.vector.scalar_tensor_tensor(grouped(ce[h][:]), spread(a_sum[h][:]), -1.0 / GROUP, grouped(a[h][:]),
+            nc.vector.scalar_tensor_tensor(grouped(ce[:, cols(h)]), spread(a_sum[h]), -1.0 / GROUP, grouped(a[h][:]),
                                            ALU.mult, ALU.add)
         ta = []
+        gdw = sb.tile([P, J], U16, name="gdw", tag="after_mean0", align_bytes=64)
         for h in hs:
-            gdw = sb.tile([P, HJ], U16, name="gdw%d" % h, tag="after_mean%d" % h, align_bytes=64)
-            nc.vector.tensor_copy(gdw[:], dw[:].indirect(offsets[:, h * HG:(h + 1) * HG]))
-            ta.append(product("ta%d" % h, gdw[:], gds[:, cols(h)]))
+            nc.vector.tensor_copy(gdw[:, cols(h)], dw[:].indirect(offsets[:, h * HG:(h + 1) * HG]))
+            ta.append(product("ta%d" % h, gdw[:, cols(h)], gds[:, cols(h)]))
+        cea = sb.tile([P, J], F32, name="cea", tag="words")
+        nc.gpsimd.tensor_tensor(cea[:], ce[:], a_sb[:], ALU.mult)
         for h in hs:
-            nc.gpsimd.tensor_tensor(grouped(e0[h][:]), spread(sm2[h][:]), grouped(x[h][:]), ALU.subtract)
-        for h in hs:
-            nc.scalar.activation(sq[h][:], ce[h][:], ACT.Square)
+            nc.scalar.activation(sq[h][:], ce[:, cols(h)], ACT.Square)
         for h in hs:
             nc.scalar.activation(den[h][:], sq[h][:], ACT.Identity, bias=1.0, scale=s_col[:])
         for h in hs:
@@ -141,12 +136,11 @@ def tile_attend_tcontrastpool_kernel(tc, dtab_words, dtab_scales, tab_words, tab
             nc.vector.scalar_tensor_tensor(grouped(tce[h][:]), spread(t_sum[h][:]), -1.0 / GROUP, grouped(ta[h][:]),
                                            ALU.mult, ALU.add)
         for h in hs:
-            nc.vector.tensor_tensor(u[h][:], tce[h][:], e0[h][:], ALU.mult)
+            nc.vector.tensor_tensor(v[h][:], ta[h][:], den[h][:], ALU.mult)
         for h in hs:
-            nc.vector.scalar_tensor_tensor(grouped(v[h][:]), spread(t_sum[h][:]), 1.0 / GROUP, grouped(den[h][:]),
-                                           ALU.mult, ALU.mult)
+            nc.vector.scalar_tensor_tensor(u[h][:], tce[h][:], s_col[:], cea[:, cols(h)], ALU.mult, ALU.mult)
         for h in hs:
-            nc.vector.tensor_tensor(n[h][:], u[h][:], v[h][:], ALU.add)
+            nc.vector.scalar_tensor_tensor(n[h][:], u[h][:], -2.0, v[h][:], ALU.mult, ALU.add)
         for h in hs:
             nc.vector.scalar_tensor_tensor(y1[h][:], n[h][:], og_col[:], q4[h][:], ALU.mult, ALU.mult)
         for h in hs:

@@ -42,51 +42,43 @@ def tile_attend_tcontrastpool_kernel(tc, dtab_words, dtab_scales, tab_words, tab
         def cols(h):
             return slice(h * HJ, (h + 1) * HJ)
 
-        def load_scales(queue, tile, scales):
-            for q in (0, 2, 1, 3):
-                queue.dma_start(tile[32 * q:32 * q + 4, :].bitcast(I32), scales[0, 4 * q:4 * q + 4, :].bitcast(I32))
-
         hs = range(HALVES)
         offsets = sb.tile([P, J // 16], U16, name="offsets")
         nc.sync.dma_start(offsets[:], offs)
 
-        tw = sb.tile([P, T], U16, name="tw", tag="words")
-        ts = sb.tile([P, T], U8, name="ts")
-        s_col = sb.tile([P, 1], F32, name="s_col")
-        og_col = sb.tile([P, 1], F32, name="og_col")
-        warm_in = sb.tile([P, 1], F32, name="warm_in", tag="after_warm_in")
-        warm_out = sb.tile([P, 1], F32, name="warm_out", tag="after_warm_out", align_bytes=64)
+        ts = sb.tile([P, T], U8, name="ts", tag="tab_scales")
+        ds = sb.tile([P, T], U8, name="ds", tag="dtab_scales")
+        w_raw = sb.tile([P, PACK * R], F32, name="w_raw")
+        warm_in = sb.tile([P, 1], F32, name="warm_in", tag="tab_words")
+        warm_out = sb.tile([P, 1], F32, name="warm_out", tag="dtab_words")
 
+        nc.scalar.dma_start(w_raw[:], w1.rearrange("(p j) r -> p (j r)", j=PACK))
         nc.vector.memset(ts[:].bitcast(I32), 0)
+        nc.vector.memset(ds[:].bitcast(I32), 0)
         nc.vector.memset(warm_in[:], 1.0)
-        nc.sync.dma_start(tw[:].bitcast(I32), tab_words[0].bitcast(I32))
-        load_scales(nc.sync, ts, tab_scales)
-        nc.gpsimd.dma_start(s_col[:], sharp)
-        nc.gpsimd.dma_start(og_col[:], og)
+        nc.sync.dma_start(ts[0:16, :].bitcast(I32), tab_scales[0].bitcast(I32))
+        nc.sync.dma_start(ds[0:16, :].bitcast(I32), dtab_scales[0].bitcast(I32))
 
         nc.scalar.activation(warm_out[:], warm_in[:], ACT.Abs_reciprocal_sqrt)
-        w_raw = sb.tile([P, PACK * R], F32, name="w_raw", tag="after_warm_in")
-        nc.sync.dma_start(w_raw[:], w1.rearrange("(p j) r -> p (j r)", j=PACK))
-        ds = sb.tile([P, T], U8, name="ds", tag="after_warm_out", align_bytes=64)
-        nc.vector.memset(ds[:].bitcast(I32), 0)
-        load_scales(nc.scalar, ds, dtab_scales)
+        tw = sb.tile([P, T], U16, name="tw", tag="tab_words")
+        dw = sb.tile([P, T], U16, name="dw", tag="dtab_words")
+        nc.sync.dma_start(tw[:].bitcast(I32), tab_words[0].bitcast(I32))
+        nc.sync.dma_start(dw[:].bitcast(I32), dtab_words[0].bitcast(I32))
 
         w_bf = sb.tile([P, R, PACK], BF16, name="w_bf", align_bytes=64)
         nc.scalar.copy(w_bf[:], w_raw[:].rearrange("p (j r) -> p r j", j=PACK))
 
-        gtw = sb.tile([P, J], U16, name="gtw", tag="after_a", align_bytes=64)
-        gts = sb.tile([P, J], U8, name="gts", align_bytes=64)
+        gts = sb.tile([P, J], U8, name="gts")
+        gds = sb.tile([P, J], U8, name="gds")
+        gtw = sb.tile([P, J], U16, name="gtw", align_bytes=64)
         w_codes = sb.tile([P, R], U32, name="w_codes", align_bytes=64)
         w_scales = sb.tile([P, R], U8, name="w_scales", align_bytes=64)
 
-        nc.vector.tensor_copy(gtw[:], tw[:].indirect(offsets[:]))
-        dw = sb.tile([P, T], U16, name="dw", tag="words")
-        nc.sync.dma_start(dw[:].bitcast(I32), dtab_words[0].bitcast(I32))
-        nc.vector.tensor_copy(gts[:], ts[:].indirect(offsets[:]))
-        nc.vector.quantize_mx(out=w_codes[:].bitcast(FP8X4), scales=w_scales[:],
-                              in_=w_bf[:].rearrange("p r j -> p (r j)"))
-        gds = sb.tile([P, J], U8, name="gds", align_bytes=64)
-        nc.vector.tensor_copy(gds[:], ds[:].indirect(offsets[:]))
+        def place(queue, name, rows):
+            plane = sb.tile([P, J], U8, name=name, align_bytes=64)
+            for q in range(4):
+                queue.dma_start(plane[32 * q:32 * q + 4, :].bitcast(I32), rows[4 * q:4 * q + 4, :].bitcast(I32))
+            return plane
 
         def product(name, words, scales):
             bank = ps.tile([P, HJ], F32, name=name)
@@ -94,8 +86,22 @@ def tile_attend_tcontrastpool_kernel(tc, dtab_words, dtab_scales, tab_words, tab
                                 rhs=words.bitcast(FP4X4), rhs_scale=scales, start=True, stop=True)
             return bank
 
-        a = [product("a%d" % h, gtw[:, cols(h)], gts[:, cols(h)]) for h in hs]
-        base_sb = sb.tile([P, J], F32, name="base_sb", tag="after_a", align_bytes=64)
+        nc.vector.tensor_copy(gts[:], ts[:].indirect(offsets[:]))
+        t_plane = place(nc.scalar, "t_plane", gts)
+        nc.vector.tensor_copy(gds[:], ds[:].indirect(offsets[:]))
+        d_plane = place(nc.sync, "d_plane", gds)
+        s_col = sb.tile([P, 1], F32, name="s_col", tag="tab_scales")
+        og_col = sb.tile([P, 1], F32, name="og_col", tag="dtab_scales")
+        nc.sync.dma_start(s_col[:], sharp)
+        nc.sync.dma_start(og_col[:], og)
+        nc.vector.quantize_mx(out=w_codes[:].bitcast(FP8X4), scales=w_scales[:],
+                              in_=w_bf[:].rearrange("p r j -> p (r j)"))
+        nc.vector.tensor_copy(gtw[:], tw[:].indirect(offsets[:]))
+        a = [product("a%d" % h, gtw[:, cols(h)], t_plane[:, cols(h)]) for h in hs]
+        gdw0 = sb.tile([P, HJ], U16, name="gdw0", align_bytes=64)
+        nc.vector.tensor_copy(gdw0[:], dw[:].indirect(offsets[:, 0:HG]))
+        ta = [product("ta0", gdw0[:], d_plane[:, cols(0)])]
+        base_sb = sb.tile([P, J], F32, name="base_sb", tag="tab_words")
         nc.sync.dma_start(base_sb[:], base)
 
         a_sb = sb.tile([P, J], F32, name="a_sb")
@@ -107,18 +113,16 @@ def tile_attend_tcontrastpool_kernel(tc, dtab_words, dtab_scales, tab_words, tab
         t_sum = [sb.tile([P, HG], F32, name="t_sum%d" % h) for h in hs]
 
         for h in hs:
-            nc.scalar.copy(a_sb[:, cols(h)], a[h][:])
-        for h in hs:
             nc.vector.tensor_reduce(a_sum[h], grouped(a[h][:]), AX.X, ALU.add)
         for h in hs:
             nc.vector.scalar_tensor_tensor(grouped(ce[:, cols(h)]), spread(a_sum[h]), -1.0 / GROUP, grouped(a[h][:]),
                                            ALU.mult, ALU.add)
-        ta = []
-        gdw = sb.tile([P, J], U16, name="gdw", tag="after_mean0", align_bytes=64)
         for h in hs:
-            nc.vector.tensor_copy(gdw[:, cols(h)], dw[:].indirect(offsets[:, h * HG:(h + 1) * HG]))
-            ta.append(product("ta%d" % h, gdw[:, cols(h)], gds[:, cols(h)]))
-        cea = sb.tile([P, J], F32, name="cea", tag="words")
+            nc.scalar.copy(a_sb[:, cols(h)], a[h][:])
+        gdw1 = sb.tile([P, HJ], U16, name="gdw1", tag="after_mean0", align_bytes=64)
+        nc.vector.tensor_copy(gdw1[:], dw[:].indirect(offsets[:, HG:G]))
+        ta.append(product("ta1", gdw1[:], d_plane[:, cols(1)]))
+        cea = sb.tile([P, J], F32, name="cea", tag="dtab_words")
         nc.gpsimd.tensor_tensor(cea[:], ce[:], a_sb[:], ALU.mult)
         for h in hs:
             nc.scalar.activation(sq[h][:], ce[:, cols(h)], ACT.Square)

from contextlib import ExitStack

import concourse.mybir as mybir

K, R, T, J, G = 512, 128, 2048, 512, 32
P = 128
PACK = 4
GROUP = J // G
HALVES = 2
HJ = J // HALVES
HG = G // HALVES
FLOPS = 2 * 2 * K * R * J

F32 = mybir.dt.float32
BF16 = mybir.dt.bfloat16
I32 = mybir.dt.int32
U32 = mybir.dt.uint32
U16 = mybir.dt.uint16
U8 = mybir.dt.uint8
FP8X4 = mybir.dt.float8_e4m3fn_x4
FP4X4 = mybir.dt.float4_e2m1fn_x4
ALU = mybir.AluOpType
ACT = mybir.ActivationFunctionType
AX = mybir.AxisListType


def tile_attend_tcontrastpool_kernel(tc, dtab_words, dtab_scales, tab_words, tab_scales, w1, sharp, og, base, offs, out):
    nc = tc.nc
    with ExitStack() as ctx:
        sb = ctx.enter_context(tc.tile_pool(name="sb", bufs=1))
        ps = ctx.enter_context(tc.psum_pool(name="ps", bufs=1))

        def halves(name):
            return [sb.tile([P, HJ], F32, name="%s%d" % (name, h)) for h in range(HALVES)]

        def grouped(ap):
            return ap.rearrange("p (g i) -> p g i", i=GROUP)

        def spread(ap):
            return ap.unsqueeze(2).to_broadcast([P, HG, GROUP])

        def cols(h):
            return slice(h * HJ, (h + 1) * HJ)

        hs = range(HALVES)
        offsets = sb.tile([P, J // 16], U16, name="offsets")
        nc.sync.dma_start(offsets[:], offs)

        ts = sb.tile([P, T], U8, name="ts", tag="tab_scales")
        ds = sb.tile([P, T], U8, name="ds", tag="dtab_scales")
        w_raw = sb.tile([P, PACK * R], F32, name="w_raw")
        warm_in = sb.tile([P, 1], F32, name="warm_in", tag="tab_words")
        warm_out = sb.tile([P, 1], F32, name="warm_out", tag="dtab_words")

        nc.scalar.dma_start(w_raw[:], w1.rearrange("(p j) r -> p (j r)", j=PACK))
        nc.vector.memset(ts[:].bitcast(I32), 0)
        nc.vector.memset(ds[:].bitcast(I32), 0)
        nc.vector.memset(warm_in[:], 1.0)
        nc.sync.dma_start(ts[0:16, :].bitcast(I32), tab_scales[0].bitcast(I32))
        nc.sync.dma_start(ds[0:16, :].bitcast(I32), dtab_scales[0].bitcast(I32))

        nc.scalar.activation(warm_out[:], warm_in[:], ACT.Abs_reciprocal_sqrt)
        tw = sb.tile([P, T], U16, name="tw", tag="tab_words")
        dw = sb.tile([P, T], U16, name="dw", tag="dtab_words")
        nc.sync.dma_start(tw[:].bitcast(I32), tab_words[0].bitcast(I32))
        nc.sync.dma_start(dw[:].bitcast(I32), dtab_words[0].bitcast(I32))

        w_bf = sb.tile([P, R, PACK], BF16, name="w_bf", align_bytes=64)
        nc.scalar.copy(w_bf[:], w_raw[:].rearrange("p (j r) -> p r j", j=PACK))

        gts = sb.tile([P, J], U8, name="gts")
        gds = sb.tile([P, J], U8, name="gds")
        gtw = sb.tile([P, J], U16, name="gtw", align_bytes=64)
        w_codes = sb.tile([P, R], U32, name="w_codes", align_bytes=64)
        w_scales = sb.tile([P, R], U8, name="w_scales", align_bytes=64)

        def place(queue, name, rows):
            plane = sb.tile([P, J], U8, name=name, align_bytes=64)
            for q in range(4):
                queue.dma_start(plane[32 * q:32 * q + 4, :].bitcast(I32), rows[4 * q:4 * q + 4, :].bitcast(I32))
            return plane

        def product(name, words, scales):
            bank = ps.tile([P, HJ], F32, name=name)
            nc.tensor.matmul_mx(out=bank[:], lhsT=w_codes[:].bitcast(FP8X4), lhsT_scale=w_scales[:],
                                rhs=words.bitcast(FP4X4), rhs_scale=scales, start=True, stop=True)
            return bank

        nc.vector.tensor_copy(gts[:], ts[:].indirect(offsets[:]))
        t_plane = place(nc.scalar, "t_plane", gts)
        nc.vector.tensor_copy(gds[:], ds[:].indirect(offsets[:]))
        d_plane = place(nc.sync, "d_plane", gds)
        s_col = sb.tile([P, 1], F32, name="s_col", tag="tab_scales")
        og_col = sb.tile([P, 1], F32, name="og_col", tag="dtab_scales")
        nc.sync.dma_start(s_col[:], sharp)
        nc.sync.dma_start(og_col[:], og)
        nc.vector.quantize_mx(out=w_codes[:].bitcast(FP8X4), scales=w_scales[:],
                              in_=w_bf[:].rearrange("p r j -> p (r j)"))
        nc.vector.tensor_copy(gtw[:], tw[:].indirect(offsets[:]))
        a = [product("a%d" % h, gtw[:, cols(h)], t_plane[:, cols(h)]) for h in hs]
        gdw0 = sb.tile([P, HJ], U16, name="gdw0", align_bytes=64)
        nc.vector.tensor_copy(gdw0[:], dw[:].indirect(offsets[:, 0:HG]))
        ta = [product("ta0", gdw0[:], d_plane[:, cols(0)])]
        base_sb = sb.tile([P, J], F32, name="base_sb", tag="tab_words")
        nc.sync.dma_start(base_sb[:], base)

        a_sb = sb.tile([P, J], F32, name="a_sb")
        ce = sb.tile([P, J], F32, name="ce")
        sq, den = halves("sq"), halves("den")
        q1, q2, q4 = halves("q1"), halves("q2"), halves("q4")
        tce, u, v, n, y1, y = halves("tce"), halves("u"), halves("v"), halves("n"), halves("y1"), halves("y")
        a_sum = [sb.tile([P, HG], F32, name="a_sum%d" % h, tag="after_mean%d" % h, align_bytes=64)[:] for h in hs]
        t_sum = [sb.tile([P, HG], F32, name="t_sum%d" % h) for h in hs]

        for h in hs:
            nc.vector.tensor_reduce(a_sum[h], grouped(a[h][:]), AX.X, ALU.add)
        for h in hs:
            nc.vector.scalar_tensor_tensor(grouped(ce[:, cols(h)]), spread(a_sum[h]), -1.0 / GROUP, grouped(a[h][:]),
                                           ALU.mult, ALU.add)
        for h in hs:
            nc.scalar.copy(a_sb[:, cols(h)], a[h][:])
        gdw1 = sb.tile([P, HJ], U16, name="gdw1", tag="after_mean0", align_bytes=64)
        nc.vector.tensor_copy(gdw1[:], dw[:].indirect(offsets[:, HG:G]))
        ta.append(product("ta1", gdw1[:], d_plane[:, cols(1)]))
        cea = sb.tile([P, J], F32, name="cea", tag="dtab_words")
        nc.gpsimd.tensor_tensor(cea[:], ce[:], a_sb[:], ALU.mult)
        for h in hs:
            nc.scalar.activation(sq[h][:], ce[:, cols(h)], ACT.Square)
        for h in hs:
            nc.scalar.activation(den[h][:], sq[h][:], ACT.Identity, bias=1.0, scale=s_col[:])
        for h in hs:
            nc.scalar.activation(q1[h][:], den[h][:], ACT.Abs_reciprocal_sqrt)
        for h in hs:
            nc.scalar.activation(q2[h][:], q1[h][:], ACT.Square)
        for h in hs:
            nc.scalar.activation(q4[h][:], q2[h][:], ACT.Square)
        for h in hs:
            nc.vector.tensor_reduce(t_sum[h][:], grouped(ta[h][:]), AX.X, ALU.add)
        for h in hs:
            nc.vector.scalar_tensor_tensor(grouped(tce[h][:]), spread(t_sum[h][:]), -1.0 / GROUP, grouped(ta[h][:]),
                                           ALU.mult, ALU.add)
        for h in hs:
            nc.vector.tensor_tensor(v[h][:], ta[h][:], den[h][:], ALU.mult)
        for h in hs:
            nc.vector.scalar_tensor_tensor(u[h][:], tce[h][:], s_col[:], cea[:, cols(h)], ALU.mult, ALU.mult)
        for h in hs:
            nc.vector.scalar_tensor_tensor(n[h][:], u[h][:], -2.0, v[h][:], ALU.mult, ALU.add)
        for h in hs:
            nc.vector.scalar_tensor_tensor(y1[h][:], n[h][:], og_col[:], q4[h][:], ALU.mult, ALU.mult)
        for h in hs:
            nc.vector.tensor_tensor(y[h][:], y1[h][:], base_sb[:, cols(h)], ALU.add)
            nc.sync.dma_start(out[:, cols(h)], y[h][:])
